import numpy as np, ml_dtypes
CORES = [35,38,43,46]
N = 4
import mx_ref
NC, G = 128, 2
C = np.float32(0.0133)
FROM = [[1,2,3,0],[3,2,0,1],[3,2,1,0]]
BF = ml_dtypes.bfloat16
def cut(t, i, w=512):
    return t[:, w * i:w * i + w]
def tile(rs):
    return np.stack(rs, axis=2).reshape(128, -1).astype(BF)
def layer(w, X):
    out = []
    for i in range(G):
        for t in range(len(X)):
            p = mx_ref.matmul(mx_ref.quantize(cut(w, len(X) * i + t)), X[t])
            z = p if t == 0 else z + p
        out.append(z)
    return out
def act(Z):
    return [np.maximum(s * z, 0) * C for z in Z for s in (1, -1)]
def setup_inputs(rng):
    def f(*shape):
        return mx_ref.flush((rng.standard_normal(shape, dtype=np.float32) * np.exp2(rng.integers(-2, 3, shape[:-1] + (1,)))).astype(BF))
    return {"x": f(N, 128, 4 * NC), "w": f(N, 128, 2 * 2 * G * 512), "v": f(N, 128, 2 * 512)}
def setup_inputs_blocks(rng):
    d = setup_inputs(rng)
    for k in ("x", "v"): d[k] = mx_ref.spread(d[k], rng, 4)
    for k in ("w",): d[k] = mx_ref.spread(d[k], rng, 2)
    return d
def setup_inputs_wide(rng):
    d = setup_inputs(rng)
    for k in ("x", "w", "v"): d[k] = mx_ref.flush((d[k].astype(np.float32) * np.exp2(rng.integers(-5, 6, (N, 1, 1))).astype(np.float32)).astype(BF))
    return d
def reference(x, w, v):
    a = [mx_ref.quantize(x[r]) for r in range(N)]
    for l in range(2):
        a = [mx_ref.quantize(tile(act(layer(cut(w[r], l, 2 * G * 512), [a[r], a[FROM[l][r]]])))) for r in range(N)]
    y = np.zeros((N, 128, NC), np.float32)
    for r in range(N):
        y[r] = mx_ref.matmul(mx_ref.quantize(cut(v[r], 0)), a[r]) + mx_ref.matmul(mx_ref.quantize(cut(v[r], 1)), a[FROM[2][r]])
    return {"y": y}

@@ -1,0 +1,114 @@
+import numpy as np
+from concourse.mybir import dt, AluOpType, ActivationFunctionType
+
+NC = 128
+TW = 4 * NC
+C = float(np.float32(0.0133))
+CODES, PLANE = "float8_e4m3fn_x4", "uint8"
+
+SCRATCH = {
+    "xs": ("sbuf", [128, TW], "bfloat16"),
+    "ws0": ("sbuf", [128, 4 * TW], "bfloat16"), "ws1": ("sbuf", [128, 4 * TW], "bfloat16"),
+    "vs": ("sbuf", [128, 2 * TW], "bfloat16"),
+    "wc0": ("sbuf", [128, 4 * NC], CODES), "wp0": ("sbuf", [128, 4 * NC], PLANE),
+    "wc1": ("sbuf", [128, 4 * NC], CODES), "wp1": ("sbuf", [128, 4 * NC], PLANE),
+    "vc": ("sbuf", [128, 2 * NC], CODES), "vp": ("sbuf", [128, 2 * NC], PLANE),
+    "h1": ("sbuf", [128, TW], "bfloat16"), "h2": ("sbuf", [128, TW], "bfloat16"),
+    "ps": ("psum", [128, 512 * 5], "float32"),
+    "ysb": ("sbuf", [128, NC], "float32"),
+}
+for _l in range(3):
+    for _n in ("a", "b"):
+        SCRATCH["%s%dc" % (_n, _l)] = ("sbuf", [128, NC], CODES)
+        SCRATCH["%s%dp" % (_n, _l)] = ("sbuf", [128, NC], PLANE)
+
+SEMAPHORES = ["ldx", "ldw0", "ldw1", "ldv", "qa0", "qa1", "qa2", "qw0", "qw1", "qv", "arr0", "arr1", "arr2",
+              "z00", "z01", "z10", "z11", "hs0", "hs1", "zy", "yc", "sty", "sent"]
+
+
+def _takers(T, l, r):
+    return [T.cores[q] for q in range(len(T.cores)) if T.tables["FROM"][l][q] == r]
+
+
+def _engines(T, topo, r):
+    m = None
+    for l in range(3):
+        for d in _takers(T, l, r):
+            if not topo.may_write(T.cores[r], d):
+                raise ValueError("no direct write from core %d to core %d" % (T.cores[r], d))
+            m = topo.mask(T.cores[r], d) if m is None else m & topo.mask(T.cores[r], d)
+    return m, bin(m).count("1")
+
+
+def rank_program(g, core, T, topo):
+    r = T.rank_of(core)
+    if r is None:
+        return
+    S, V, A, PE = T.sem, g.vector, g.scalar, g.tensor
+    FROM = T.tables["FROM"]
+    bank = lambda b: T.ps[:, 512 * b:512 * b + NC]
+    col = lambda t, k: t[:, NC * k:NC * k + NC]
+
+    for q, lo, hi in ((g.sync, 0, 64), (g.scalar, 64, 128)):
+        q.dma_start(T.xs[lo:hi, :], T.x[lo:hi, :]).then_inc(S.ldx, 16)
+        q.dma_start(T.ws0[lo:hi, :], T.w[lo:hi, 0:4 * TW]).then_inc(S.ldw0, 16)
+        q.dma_start(T.ws1[lo:hi, :], T.w[lo:hi, 4 * TW:8 * TW]).then_inc(S.ldw1, 16)
+        q.dma_start(T.vs[lo:hi, :], T.v[lo:hi, :]).then_inc(S.ldv, 16)
+
+    mask, ne = _engines(T, topo, r)
+    left = 0
+    for l in range(3):
+        g.wait_ge(S["qa%d" % l], 1)
+        for d in _takers(T, l, r):
+            rid, pid, _ = topo.addr(d)
+            g.remote_dma(out_ap=T["b%dc" % l][:].bitcast(dt.uint8), in_ap=T["a%dc" % l][:].bitcast(dt.uint8),
+                         remote_sem=S["arr%d" % l], local_sem=S.sent, pid=pid, routing_id=rid, dma_engine_mask=mask)
+            g.remote_dma(out_ap=T["b%dp" % l][:], in_ap=T["a%dp" % l][:],
+                         remote_sem=S["arr%d" % l], local_sem=S.sent, pid=pid, routing_id=rid, dma_engine_mask=mask)
+            left += 2 * ne
+    g.wait_ge(S.sent, left)
+
+    landed = [2 * _engines(T, topo, FROM[l][r])[1] for l in range(3)]
+
+    V.wait_ge(S.ldx, 32)
+    V.quantize_mx(T.a0c[:], T.a0p[:], T.xs[:]).then_inc(S.qa0, 1)
+    V.wait_ge(S.ldw0, 32)
+    V.quantize_mx(T.wc0[:], T.wp0[:], T.ws0[:]).then_inc(S.qw0, 1)
+
+    for l in range(2):
+        wc, wp, h = T["wc%d" % l], T["wp%d" % l], T["h%d" % (l + 1)]
+        z = [S["z%d%d" % (l, i)] for i in range(2)]
+        hs = S["hs%d" % l]
+        PE.wait_ge(S["qa%d" % l], 1)
+        PE.wait_ge(S["qw%d" % l], 1)
+        for i in range(2):
+            PE.matmul_mx(bank(2 * l + i), col(wc, 2 * i), col(wp, 2 * i), T["a%dc" % l][:], T["a%dp" % l][:], True, False)
+        PE.wait_ge(S["arr%d" % l], landed[l])
+        for i in range(2):
+            PE.matmul_mx(bank(2 * l + i), col(wc, 2 * i + 1), col(wp, 2 * i + 1), T["b%dc" % l][:], T["b%dp" % l][:],
+                         False, True).then_inc(z[i], 1)
+        V.wait_ge(z[0], 1)
+        V.tensor_scalar(h[:, 0:TW:4], bank(2 * l), 0.0, C, AluOpType.max, AluOpType.mult).then_inc(hs, 1)
+        V.tensor_scalar(h[:, 1:TW:4], bank(2 * l), -C, 0.0, AluOpType.mult, AluOpType.max).then_inc(hs, 1)
+        A.wait_ge(z[1], 1)
+        A.activation(h[:, 2:TW:4], bank(2 * l + 1), ActivationFunctionType.Relu, scale=C).then_inc(hs, 1)
+        A.activation(h[:, 3:TW:4], bank(2 * l + 1), ActivationFunctionType.Relu, scale=-C).then_inc(hs, 1)
+        V.wait_ge(hs, 4)
+        V.quantize_mx(T["a%dc" % (l + 1)][:], T["a%dp" % (l + 1)][:], h[:]).then_inc(S["qa%d" % (l + 1)], 1)
+        if l == 0:
+            V.wait_ge(S.ldw1, 32)
+            V.quantize_mx(T.wc1[:], T.wp1[:], T.ws1[:]).then_inc(S.qw1, 1)
+        else:
+            V.wait_ge(S.ldv, 32)
+            V.quantize_mx(T.vc[:], T.vp[:], T.vs[:]).then_inc(S.qv, 1)
+
+    PE.wait_ge(S.qa2, 1)
+    PE.wait_ge(S.qv, 1)
+    PE.matmul_mx(bank(4), col(T.vc, 0), col(T.vp, 0), T.a2c[:], T.a2p[:], True, False)
+    PE.wait_ge(S.arr2, landed[2])
+    PE.matmul_mx(bank(4), col(T.vc, 1), col(T.vp, 1), T.b2c[:], T.b2p[:], False, True).then_inc(S.zy, 1)
+    V.wait_ge(S.zy, 1)
+    V.tensor_copy(T.ysb[:], bank(4)).then_inc(S.yc, 1)
+    g.sync.wait_ge(S.yc, 1)
+    g.sync.dma_start(T.y[:], T.ysb[:]).then_inc(S.sty, 16)
+    g.sync.wait_ge(S.sty, 16)

@@ -1,8 +1,10 @@
 import numpy as np
+from concourse.bass import DstId, RemoteDMATransfer
 from concourse.mybir import dt, AluOpType, ActivationFunctionType
 
 NC = 128
 TW = 4 * NC
+NR = 4
 C = float(np.float32(0.0133))
 CODES, PLANE = "float8_e4m3fn_x4", "uint8"
 
@@ -12,32 +14,64 @@ SCRATCH = {
     "vs": ("sbuf", [128, 2 * TW], "bfloat16"),
     "wc0": ("sbuf", [128, 4 * NC], CODES), "wp0": ("sbuf", [128, 4 * NC], PLANE),
     "wc1": ("sbuf", [128, 4 * NC], CODES), "wp1": ("sbuf", [128, 4 * NC], PLANE),
+    "uc1": ("sbuf", [128, 4 * NC], CODES), "up1": ("sbuf", [128, 4 * NC], PLANE),
     "vc": ("sbuf", [128, 2 * NC], CODES), "vp": ("sbuf", [128, 2 * NC], PLANE),
-    "h1": ("sbuf", [128, TW], "bfloat16"), "h2": ("sbuf", [128, TW], "bfloat16"),
-    "ps": ("psum", [128, 512 * 5], "float32"),
+    "h1": ("sbuf", [128, TW], "bfloat16"), "h20": ("sbuf", [128, TW], "bfloat16"), "h21": ("sbuf", [128, TW], "bfloat16"),
+    "ps": ("psum", [128, 512 * 7], "float32"),
     "ysb": ("sbuf", [128, NC], "float32"),
 }
-for _l in range(3):
-    for _n in ("a", "b"):
-        SCRATCH["%s%dc" % (_n, _l)] = ("sbuf", [128, NC], CODES)
-        SCRATCH["%s%dp" % (_n, _l)] = ("sbuf", [128, NC], PLANE)
+for _n in ["a0", "a1", "b0", "a20", "a21"] + ["c%d" % _p for _p in range(NR)]:
+    SCRATCH[_n + "c"] = ("sbuf", [128, NC], CODES)
+    SCRATCH[_n + "p"] = ("sbuf", [128, NC], PLANE)
 
-SEMAPHORES = ["ldx", "ldw0", "ldw1", "ldv", "qa0", "qa1", "qa2", "qw0", "qw1", "qv", "arr0", "arr1", "arr2",
-              "z00", "z01", "z10", "z11", "hs0", "hs1", "zy", "yc", "sty", "sent"]
-
-
-def _takers(T, l, r):
-    return [T.cores[q] for q in range(len(T.cores)) if T.tables["FROM"][l][q] == r]
+SEMAPHORES = ["ldx", "ldw0", "ldw1", "ldv", "qa0", "qa1", "qa20", "qa21", "qw0", "qw1", "qv", "arr0", "arrw",
+              "z00", "z01", "zj00", "zj01", "zj10", "zj11", "hs0", "hj0", "hj1", "zy", "yc", "sty", "sent"] + \
+             ["arr1_%d" % _p for _p in range(NR)]
 
 
-def _engines(T, topo, r):
-    m = None
-    for l in range(3):
-        for d in _takers(T, l, r):
-            if not topo.may_write(T.cores[r], d):
-                raise ValueError("no direct write from core %d to core %d" % (T.cores[r], d))
-            m = topo.mask(T.cores[r], d) if m is None else m & topo.mask(T.cores[r], d)
-    return m, bin(m).count("1")
+def _plan(T, p):
+    F, n = T.tables["FROM"], len(T.cores)
+    t0 = [q for q in range(n) if F[0][q] == p and q != p]
+    tw = [q for q in range(n) if F[2][q] == p and q != p]
+    w1 = [q for q in range(n) if F[1][q] == p and q != p]
+    w2 = [q for q in range(n) if q != p and q not in w1 and p in (F[2][q], F[1][F[2][q]])]
+    return t0, tw, w1, w2
+
+
+def _mask(T, topo, p, q):
+    src = T.cores[p]
+    narrow = None
+    for lst in _plan(T, p):
+        for d in lst:
+            if not topo.may_write(src, T.cores[d]):
+                raise ValueError("no direct write from core %d to core %d" % (src, T.cores[d]))
+            m = topo.mask(src, T.cores[d])
+            narrow = m if narrow is None else narrow & m
+    rest = topo.mask(src, T.cores[q]) & ~narrow
+    return rest if rest else narrow
+
+
+def _bits(m):
+    return bin(m).count("1")
+
+
+def _send(g, T, topo, p, takers, out_ap, in_ap, sem):
+    if len(takers) == 1:
+        rid, pid, _ = topo.addr(T.cores[takers[0]])
+        m = _mask(T, topo, p, takers[0])
+        g.remote_dma(out_ap=out_ap, in_ap=in_ap, remote_sem=sem, local_sem=T.sem.sent, pid=pid, routing_id=rid,
+                     dma_engine_mask=m)
+        return _bits(m)
+    groups = {}
+    for q in takers:
+        groups.setdefault(_mask(T, topo, p, q), []).append(q)
+    trs = []
+    for m, qs in groups.items():
+        ids = [DstId(rid=topo.addr(T.cores[q])[0], pnc=topo.addr(T.cores[q])[1]) for q in qs]
+        trs.append(RemoteDMATransfer(dst_ids=ids, dma_engine_mask=m, remote_sem=sem, srcs=[in_ap],
+                                     dsts=[out_ap for _ in qs]))
+    g.remote_dma_fused(trs, local_sem=T.sem.sent)
+    return sum(_bits(m) for m in groups)
 
 
 def rank_program(g, core, T, topo):
@@ -45,9 +79,12 @@ def rank_program(g, core, T, topo):
     if r is None:
         return
     S, V, A, PE = T.sem, g.vector, g.scalar, g.tensor
-    FROM = T.tables["FROM"]
+    F = T.tables["FROM"]
+    s = F[2][r]
     bank = lambda b: T.ps[:, 512 * b:512 * b + NC]
     col = lambda t, k: t[:, NC * k:NC * k + NC]
+    u8 = lambda t: t[:].bitcast(dt.uint8)
+    landed = lambda p: 2 * _bits(_mask(T, topo, p, r))
 
     for q, lo, hi in ((g.sync, 0, 64), (g.scalar, 64, 128)):
         q.dma_start(T.xs[lo:hi, :], T.x[lo:hi, :]).then_inc(S.ldx, 16)
@@ -55,60 +92,83 @@ def rank_program(g, core, T, topo):
         q.dma_start(T.ws1[lo:hi, :], T.w[lo:hi, 4 * TW:8 * TW]).then_inc(S.ldw1, 16)
         q.dma_start(T.vs[lo:hi, :], T.v[lo:hi, :]).then_inc(S.ldv, 16)
 
-    mask, ne = _engines(T, topo, r)
+    t0, tw, w1, w2 = _plan(T, r)
     left = 0
-    for l in range(3):
-        g.wait_ge(S["qa%d" % l], 1)
-        for d in _takers(T, l, r):
-            rid, pid, _ = topo.addr(d)
-            g.remote_dma(out_ap=T["b%dc" % l][:].bitcast(dt.uint8), in_ap=T["a%dc" % l][:].bitcast(dt.uint8),
-                         remote_sem=S["arr%d" % l], local_sem=S.sent, pid=pid, routing_id=rid, dma_engine_mask=mask)
-            g.remote_dma(out_ap=T["b%dp" % l][:], in_ap=T["a%dp" % l][:],
-                         remote_sem=S["arr%d" % l], local_sem=S.sent, pid=pid, routing_id=rid, dma_engine_mask=mask)
-            left += 2 * ne
+    g.wait_ge(S.qa0, 1)
+    if t0:
+        left += _send(g, T, topo, r, t0, u8(T.b0c), u8(T.a0c), S.arr0)
+        left += _send(g, T, topo, r, t0, T.b0p[:], T.a0p[:], S.arr0)
+    g.wait_ge(S.qw1, 1)
+    if tw:
+        left += _send(g, T, topo, r, tw, u8(T.uc1), u8(T.wc1), S.arrw)
+        left += _send(g, T, topo, r, tw, T.up1[:], T.wp1[:], S.arrw)
+    g.wait_ge(S.qa1, 1)
+    for wave in (w1, w2):
+        if wave:
+            left += _send(g, T, topo, r, wave, u8(T["c%dc" % r]), u8(T.a1c), S["arr1_%d" % r])
+            left += _send(g, T, topo, r, wave, T["c%dp" % r][:], T.a1p[:], S["arr1_%d" % r])
     g.wait_ge(S.sent, left)
-
-    landed = [2 * _engines(T, topo, FROM[l][r])[1] for l in range(3)]
 
     V.wait_ge(S.ldx, 32)
     V.quantize_mx(T.a0c[:], T.a0p[:], T.xs[:]).then_inc(S.qa0, 1)
     V.wait_ge(S.ldw0, 32)
     V.quantize_mx(T.wc0[:], T.wp0[:], T.ws0[:]).then_inc(S.qw0, 1)
+    V.wait_ge(S.ldw1, 32)
+    V.quantize_mx(T.wc1[:], T.wp1[:], T.ws1[:]).then_inc(S.qw1, 1)
 
-    for l in range(2):
-        wc, wp, h = T["wc%d" % l], T["wp%d" % l], T["h%d" % (l + 1)]
-        z = [S["z%d%d" % (l, i)] for i in range(2)]
-        hs = S["hs%d" % l]
-        PE.wait_ge(S["qa%d" % l], 1)
-        PE.wait_ge(S["qw%d" % l], 1)
-        for i in range(2):
-            PE.matmul_mx(bank(2 * l + i), col(wc, 2 * i), col(wp, 2 * i), T["a%dc" % l][:], T["a%dp" % l][:], True, False)
-        PE.wait_ge(S["arr%d" % l], landed[l])
-        for i in range(2):
-            PE.matmul_mx(bank(2 * l + i), col(wc, 2 * i + 1), col(wp, 2 * i + 1), T["b%dc" % l][:], T["b%dp" % l][:],
-                         False, True).then_inc(z[i], 1)
+    def to_tile(h, b0, z, hs, oc, op, done):
         V.wait_ge(z[0], 1)
-        V.tensor_scalar(h[:, 0:TW:4], bank(2 * l), 0.0, C, AluOpType.max, AluOpType.mult).then_inc(hs, 1)
-        V.tensor_scalar(h[:, 1:TW:4], bank(2 * l), -C, 0.0, AluOpType.mult, AluOpType.max).then_inc(hs, 1)
+        V.tensor_scalar(h[:, 0:TW:4], bank(b0), 0.0, C, AluOpType.max, AluOpType.mult).then_inc(hs, 1)
+        V.tensor_scalar(h[:, 1:TW:4], bank(b0), -C, 0.0, AluOpType.mult, AluOpType.max).then_inc(hs, 1)
         A.wait_ge(z[1], 1)
-        A.activation(h[:, 2:TW:4], bank(2 * l + 1), ActivationFunctionType.Relu, scale=C).then_inc(hs, 1)
-        A.activation(h[:, 3:TW:4], bank(2 * l + 1), ActivationFunctionType.Relu, scale=-C).then_inc(hs, 1)
+        A.activation(h[:, 2:TW:4], bank(b0 + 1), ActivationFunctionType.Relu, scale=C).then_inc(hs, 1)
+        A.activation(h[:, 3:TW:4], bank(b0 + 1), ActivationFunctionType.Relu, scale=-C).then_inc(hs, 1)
         V.wait_ge(hs, 4)
-        V.quantize_mx(T["a%dc" % (l + 1)][:], T["a%dp" % (l + 1)][:], h[:]).then_inc(S["qa%d" % (l + 1)], 1)
-        if l == 0:
-            V.wait_ge(S.ldw1, 32)
-            V.quantize_mx(T.wc1[:], T.wp1[:], T.ws1[:]).then_inc(S.qw1, 1)
-        else:
-            V.wait_ge(S.ldv, 32)
-            V.quantize_mx(T.vc[:], T.vp[:], T.vs[:]).then_inc(S.qv, 1)
+        V.quantize_mx(oc[:], op[:], h[:]).then_inc(done, 1)
 
-    PE.wait_ge(S.qa2, 1)
+    PE.wait_ge(S.qa0, 1)
+    PE.wait_ge(S.qw0, 1)
+    for i in range(2):
+        PE.matmul_mx(bank(i), col(T.wc0, 2 * i), col(T.wp0, 2 * i), T.a0c[:], T.a0p[:], True, False)
+    PE.wait_ge(S.arr0, landed(F[0][r]))
+    for i in range(2):
+        PE.matmul_mx(bank(i), col(T.wc0, 2 * i + 1), col(T.wp0, 2 * i + 1), T.b0c[:], T.b0p[:],
+                     False, True).then_inc(S["z0%d" % i], 1)
+    to_tile(T.h1, 0, [S.z00, S.z01], S.hs0, T.a1c, T.a1p, S.qa1)
+    V.wait_ge(S.ldv, 32)
+    V.quantize_mx(T.vc[:], T.vp[:], T.vs[:]).then_inc(S.qv, 1)
+
+    terms = []
+    for j, q in enumerate((r, s)):
+        for t, p in enumerate((q, F[1][q])):
+            terms.append((0 if p == r else 1 if p == F[1][r] else 2, j, t, p))
+    terms.sort()
+    seen, opened = set(), [0, 0]
+    for _, j, t, p in terms:
+        for name, val in (("qa1", 1) if p == r else ("arr1_%d" % p, landed(p)),
+                          ("qw1", 1) if j == 0 else ("arrw", landed(s))):
+            if name not in seen:
+                seen.add(name)
+                PE.wait_ge(S[name], val)
+        mc, mp = (T.a1c, T.a1p) if p == r else (T["c%dc" % p], T["c%dp" % p])
+        wc, wp = (T.wc1, T.wp1) if j == 0 else (T.uc1, T.up1)
+        opened[j] += 1
+        for i in range(2):
+            mm = PE.matmul_mx(bank(2 + 2 * j + i), col(wc, 2 * i + t), col(wp, 2 * i + t), mc[:], mp[:],
+                              opened[j] == 1, opened[j] == 2)
+            if opened[j] == 2:
+                mm.then_inc(S["zj%d%d" % (j, i)], 1)
+    for j in range(2):
+        to_tile(T["h2%d" % j], 2 + 2 * j, [S["zj%d0" % j], S["zj%d1" % j]], S["hj%d" % j],
+                T["a2%dc" % j], T["a2%dp" % j], S["qa2%d" % j])
+
     PE.wait_ge(S.qv, 1)
-    PE.matmul_mx(bank(4), col(T.vc, 0), col(T.vp, 0), T.a2c[:], T.a2p[:], True, False)
-    PE.wait_ge(S.arr2, landed[2])
-    PE.matmul_mx(bank(4), col(T.vc, 1), col(T.vp, 1), T.b2c[:], T.b2p[:], False, True).then_inc(S.zy, 1)
+    PE.wait_ge(S.qa20, 1)
+    PE.matmul_mx(bank(6), col(T.vc, 0), col(T.vp, 0), T.a20c[:], T.a20p[:], True, False)
+    PE.wait_ge(S.qa21, 1)
+    PE.matmul_mx(bank(6), col(T.vc, 1), col(T.vp, 1), T.a21c[:], T.a21p[:], False, True).then_inc(S.zy, 1)
     V.wait_ge(S.zy, 1)
-    V.tensor_copy(T.ysb[:], bank(4)).then_inc(S.yc, 1)
+    V.tensor_copy(T.ysb[:], bank(6)).then_inc(S.yc, 1)
     g.sync.wait_ge(S.yc, 1)
     g.sync.dma_start(T.y[:], T.ysb[:]).then_inc(S.sty, 16)
     g.sync.wait_ge(S.sty, 16)

import numpy as np
from concourse.bass import DstId, RemoteDMATransfer
from concourse.mybir import dt, AluOpType, ActivationFunctionType

NC = 128
TW = 4 * NC
NR = 4
C = float(np.float32(0.0133))
CODES, PLANE = "float8_e4m3fn_x4", "uint8"

SCRATCH = {
    "xs": ("sbuf", [128, TW], "bfloat16"),
    "ws0": ("sbuf", [128, 4 * TW], "bfloat16"), "ws1": ("sbuf", [128, 4 * TW], "bfloat16"),
    "vs": ("sbuf", [128, 2 * TW], "bfloat16"),
    "wc0": ("sbuf", [128, 4 * NC], CODES), "wp0": ("sbuf", [128, 4 * NC], PLANE),
    "wc1": ("sbuf", [128, 4 * NC], CODES), "wp1": ("sbuf", [128, 4 * NC], PLANE),
    "uc1": ("sbuf", [128, 4 * NC], CODES), "up1": ("sbuf", [128, 4 * NC], PLANE),
    "vc": ("sbuf", [128, 2 * NC], CODES), "vp": ("sbuf", [128, 2 * NC], PLANE),
    "h1": ("sbuf", [128, TW], "bfloat16"), "h20": ("sbuf", [128, TW], "bfloat16"), "h21": ("sbuf", [128, TW], "bfloat16"),
    "ps": ("psum", [128, 512 * 7], "float32"),
    "ysb": ("sbuf", [128, NC], "float32"),
}
for _n in ["a0", "a1", "b0", "a20", "a21"] + ["c%d" % _p for _p in range(NR)]:
    SCRATCH[_n + "c"] = ("sbuf", [128, NC], CODES)
    SCRATCH[_n + "p"] = ("sbuf", [128, NC], PLANE)

SEMAPHORES = ["ldx", "ldw0", "ldw1", "ldv", "qa0", "qa1", "qa20", "qa21", "qw0", "qw1", "qv", "arr0", "arrw",
              "z00", "z01", "zj00", "zj01", "zj10", "zj11", "hs0", "hj0", "hj1", "zy", "yc", "sty", "sent"] + \
             ["arr1_%d" % _p for _p in range(NR)]


def _plan(T, p):
    F, n = T.tables["FROM"], len(T.cores)
    t0 = [q for q in range(n) if F[0][q] == p and q != p]
    tw = [q for q in range(n) if F[2][q] == p and q != p]
    w1 = [q for q in range(n) if F[1][q] == p and q != p]
    w2 = [q for q in range(n) if q != p and q not in w1 and p in (F[2][q], F[1][F[2][q]])]
    return t0, tw, w1, w2


def _mask(T, topo, p, q):
    src = T.cores[p]
    narrow = None
    for lst in _plan(T, p):
        for d in lst:
            if not topo.may_write(src, T.cores[d]):
                raise ValueError("no direct write from core %d to core %d" % (src, T.cores[d]))
            m = topo.mask(src, T.cores[d])
            narrow = m if narrow is None else narrow & m
    rest = topo.mask(src, T.cores[q]) & ~narrow
    return rest if rest else narrow


def _bits(m):
    return bin(m).count("1")


def _send(g, T, topo, p, takers, out_ap, in_ap, sem):
    if len(takers) == 1:
        rid, pid, _ = topo.addr(T.cores[takers[0]])
        m = _mask(T, topo, p, takers[0])
        g.remote_dma(out_ap=out_ap, in_ap=in_ap, remote_sem=sem, local_sem=T.sem.sent, pid=pid, routing_id=rid,
                     dma_engine_mask=m)
        return _bits(m)
    groups = {}
    for q in takers:
        groups.setdefault(_mask(T, topo, p, q), []).append(q)
    trs = []
    for m, qs in groups.items():
        ids = [DstId(rid=topo.addr(T.cores[q])[0], pnc=topo.addr(T.cores[q])[1]) for q in qs]
        trs.append(RemoteDMATransfer(dst_ids=ids, dma_engine_mask=m, remote_sem=sem, srcs=[in_ap],
                                     dsts=[out_ap for _ in qs]))
    g.remote_dma_fused(trs, local_sem=T.sem.sent)
    return sum(_bits(m) for m in groups)


def rank_program(g, core, T, topo):
    r = T.rank_of(core)
    if r is None:
        return
    S, V, A, PE = T.sem, g.vector, g.scalar, g.tensor
    F = T.tables["FROM"]
    s = F[2][r]
    bank = lambda b: T.ps[:, 512 * b:512 * b + NC]
    col = lambda t, k: t[:, NC * k:NC * k + NC]
    u8 = lambda t: t[:].bitcast(dt.uint8)
    landed = lambda p: 2 * _bits(_mask(T, topo, p, r))

    for q, lo, hi in ((g.sync, 0, 64), (g.scalar, 64, 128)):
        q.dma_start(T.xs[lo:hi, :], T.x[lo:hi, :]).then_inc(S.ldx, 16)
        q.dma_start(T.ws0[lo:hi, :], T.w[lo:hi, 0:4 * TW]).then_inc(S.ldw0, 16)
        q.dma_start(T.ws1[lo:hi, :], T.w[lo:hi, 4 * TW:8 * TW]).then_inc(S.ldw1, 16)
        q.dma_start(T.vs[lo:hi, :], T.v[lo:hi, :]).then_inc(S.ldv, 16)

    t0, tw, w1, w2 = _plan(T, r)
    left = 0
    g.wait_ge(S.qa0, 1)
    if t0:
        left += _send(g, T, topo, r, t0, u8(T.b0c), u8(T.a0c), S.arr0)
        left += _send(g, T, topo, r, t0, T.b0p[:], T.a0p[:], S.arr0)
    g.wait_ge(S.qw1, 1)
    if tw:
        left += _send(g, T, topo, r, tw, u8(T.uc1), u8(T.wc1), S.arrw)
        left += _send(g, T, topo, r, tw, T.up1[:], T.wp1[:], S.arrw)
    g.wait_ge(S.qa1, 1)
    for wave in (w1, w2):
        if wave:
            left += _send(g, T, topo, r, wave, u8(T["c%dc" % r]), u8(T.a1c), S["arr1_%d" % r])
            left += _send(g, T, topo, r, wave, T["c%dp" % r][:], T.a1p[:], S["arr1_%d" % r])
    g.wait_ge(S.sent, left)

    V.wait_ge(S.ldx, 32)
    V.quantize_mx(T.a0c[:], T.a0p[:], T.xs[:]).then_inc(S.qa0, 1)
    V.wait_ge(S.ldw0, 32)
    V.quantize_mx(T.wc0[:], T.wp0[:], T.ws0[:]).then_inc(S.qw0, 1)
    V.wait_ge(S.ldw1, 32)
    V.quantize_mx(T.wc1[:], T.wp1[:], T.ws1[:]).then_inc(S.qw1, 1)

    def to_tile(h, b0, z, hs, oc, op, done):
        V.wait_ge(z[0], 1)
        V.tensor_scalar(h[:, 0:TW:4], bank(b0), 0.0, C, AluOpType.max, AluOpType.mult).then_inc(hs, 1)
        V.tensor_scalar(h[:, 1:TW:4], bank(b0), -C, 0.0, AluOpType.mult, AluOpType.max).then_inc(hs, 1)
        A.wait_ge(z[1], 1)
        A.activation(h[:, 2:TW:4], bank(b0 + 1), ActivationFunctionType.Relu, scale=C).then_inc(hs, 1)
        A.activation(h[:, 3:TW:4], bank(b0 + 1), ActivationFunctionType.Relu, scale=-C).then_inc(hs, 1)
        V.wait_ge(hs, 4)
        V.quantize_mx(oc[:], op[:], h[:]).then_inc(done, 1)

    PE.wait_ge(S.qa0, 1)
    PE.wait_ge(S.qw0, 1)
    for i in range(2):
        PE.matmul_mx(bank(i), col(T.wc0, 2 * i), col(T.wp0, 2 * i), T.a0c[:], T.a0p[:], True, False)
    PE.wait_ge(S.arr0, landed(F[0][r]))
    for i in range(2):
        PE.matmul_mx(bank(i), col(T.wc0, 2 * i + 1), col(T.wp0, 2 * i + 1), T.b0c[:], T.b0p[:],
                     False, True).then_inc(S["z0%d" % i], 1)
    to_tile(T.h1, 0, [S.z00, S.z01], S.hs0, T.a1c, T.a1p, S.qa1)
    V.wait_ge(S.ldv, 32)
    V.quantize_mx(T.vc[:], T.vp[:], T.vs[:]).then_inc(S.qv, 1)

    terms = []
    for j, q in enumerate((r, s)):
        for t, p in enumerate((q, F[1][q])):
            terms.append((0 if p == r else 1 if p == F[1][r] else 2, j, t, p))
    terms.sort()
    seen, opened = set(), [0, 0]
    for _, j, t, p in terms:
        for name, val in (("qa1", 1) if p == r else ("arr1_%d" % p, landed(p)),
                          ("qw1", 1) if j == 0 else ("arrw", landed(s))):
            if name not in seen:
                seen.add(name)
                PE.wait_ge(S[name], val)
        mc, mp = (T.a1c, T.a1p) if p == r else (T["c%dc" % p], T["c%dp" % p])
        wc, wp = (T.wc1, T.wp1) if j == 0 else (T.uc1, T.up1)
        opened[j] += 1
        for i in range(2):
            mm = PE.matmul_mx(bank(2 + 2 * j + i), col(wc, 2 * i + t), col(wp, 2 * i + t), mc[:], mp[:],
                              opened[j] == 1, opened[j] == 2)
            if opened[j] == 2:
                mm.then_inc(S["zj%d%d" % (j, i)], 1)
    for j in range(2):
        to_tile(T["h2%d" % j], 2 + 2 * j, [S["zj%d0" % j], S["zj%d1" % j]], S["hj%d" % j],
                T["a2%dc" % j], T["a2%dp" % j], S["qa2%d" % j])

    PE.wait_ge(S.qv, 1)
    PE.wait_ge(S.qa20, 1)
    PE.matmul_mx(bank(6), col(T.vc, 0), col(T.vp, 0), T.a20c[:], T.a20p[:], True, False)
    PE.wait_ge(S.qa21, 1)
    PE.matmul_mx(bank(6), col(T.vc, 1), col(T.vp, 1), T.a21c[:], T.a21p[:], False, True).then_inc(S.zy, 1)
    V.wait_ge(S.zy, 1)
    V.tensor_copy(T.ysb[:], bank(6)).then_inc(S.yc, 1)
    g.sync.wait_ge(S.yc, 1)
    g.sync.dma_start(T.y[:], T.ysb[:]).then_inc(S.sty, 16)
    g.sync.wait_ge(S.sty, 16)
